import numpy as np
import ml_dtypes

BF16 = ml_dtypes.bfloat16


def bf(x):
    return np.asarray(x, np.float32).astype(BF16)


def f32(x):
    return np.asarray(x, np.float32)


def f64(x):
    return np.asarray(x).astype(np.float64)


def striped(idx):
    return np.concatenate([l.reshape(-1, 16).T for l in idx])


def rows(idx, k):
    return np.tile(np.repeat(idx, 16, axis=0), (k // (16 * 8), 1))


def look(tab, idx):
    return np.take_along_axis(f64(tab), rows(idx, len(tab)), axis=1)


K, S, D, V, N, M = 512, 2048, 2, 1536, 3072, 128


def setup_inputs():
    return {"tab": bf(0.7 * np.random.standard_normal((D, K, S))), "base": bf(np.random.standard_normal((K, V))), "w": bf(np.random.standard_normal((K, M)) / np.sqrt(K)), "b": f32(0.5 * np.random.standard_normal((M, 1))), "offs": striped(np.random.randint(0, S, (8, N)))}


def reference(tab, base, w, b, offs):
    idx = np.stack([g.T.reshape(-1) for g in np.split(offs, 8)])
    x = f64(base) + sum(look(tab[d], idx[:, d * V:(d + 1) * V]) for d in range(D))
    y = f64(w).T @ x
    return np.maximum(y + f64(b), 0.0)

@@ -1,0 +1,66 @@
+import concourse.mybir as mybir
+
+P = 128
+PIECE = 512
+GROUP = 16
+
+BF16, F32, U16 = mybir.dt.bfloat16, mybir.dt.float32, mybir.dt.uint16
+ADD = mybir.AluOpType.add
+RELU = mybir.ActivationFunctionType.Relu
+
+FLOPS = 2 * 512 * 128 * 1536
+
+
+def tile_lookup_res_add_relu_kernel(tc, tab, base, w, b, offs, out):
+    nc = tc.nc
+    stages, rows, codewords = tab.shape
+    vectors = base.shape[1]
+    features = w.shape[1]
+    blocks, pieces = rows // P, vectors // PIECE
+
+    with (
+        tc.tile_pool(name="held", bufs=1) as held,
+        tc.psum_pool(name="psum", bufs=1) as psum,
+    ):
+        offsets = held.tile([P, offs.shape[1]], U16, name="offsets")
+        nc.sync.dma_start(offsets[:], offs)
+
+        windows, sums = {}, {}
+        for r in range(blocks):
+            block = slice(r * P, (r + 1) * P)
+            for d in range(stages):
+                tab_bf = held.tile([P, codewords], BF16, name=f"tab_bf_{r}_{d}")
+                nc.sync.dma_start(tab_bf[:], tab[d, block, :])
+                windows[r, d] = held.tile([P, codewords], F32, name=f"window_{r}_{d}")
+                nc.scalar.copy(windows[r, d][:], tab_bf[:])
+                if d == 0:
+                    base_bf = held.tile([P, vectors], BF16, name=f"base_bf_{r}")
+                    nc.sync.dma_start(base_bf[:], base[block, :])
+                    sums[r, 0] = held.tile([P, vectors], F32, name=f"base_f32_{r}")
+                    nc.scalar.copy(sums[r, 0][:], base_bf[:])
+                sums[r, d + 1] = held.tile([P, vectors], F32, name=f"sum_{r}_{d}")
+            if r == 0:
+                w_bf = held.tile([P, blocks, features], BF16, name="w_bf")
+                nc.sync.dma_start(w_bf[:], w.rearrange("(r p) m -> p r m", p=P))
+                w_f32 = held.tile([P, blocks, features], F32, name="w_f32")
+                nc.scalar.copy(w_f32[:], w_bf[:])
+                bias = held.tile([P, 1], F32, name="bias")
+                nc.sync.dma_start(bias[:], b)
+
+        banks = [psum.tile([P, PIECE], F32, name=f"bank_{c}") for c in range(pieces)]
+        for r in range(blocks):
+            for d in range(stages):
+                for c in range(pieces):
+                    columns = slice(c * PIECE, (c + 1) * PIECE)
+                    first = (d * vectors + c * PIECE) // GROUP
+                    picked = windows[r, d][:].indirect(offsets[:, first : first + PIECE // GROUP])
+                    nc.vector.tensor_tensor(sums[r, d + 1][:, columns], picked, sums[r, d][:, columns], ADD)
+            for c in range(pieces):
+                columns = slice(c * PIECE, (c + 1) * PIECE)
+                nc.tensor.matmul(banks[c][:], w_f32[:, r, :], sums[r, stages][:, columns],
+                                 start=r == 0, stop=r == blocks - 1)
+
+        for c in range(pieces):
+            result = held.tile([P, PIECE], F32, name=f"result_{c}")
+            nc.scalar.activation(result[:], banks[c][:], RELU, bias=bias[:])
+            nc.sync.dma_start(out[:, c * PIECE : (c + 1) * PIECE], result[:])

@@ -2,7 +2,9 @@ import concourse.mybir as mybir
 
 P = 128
 PIECE = 512
+HALF = 256
 GROUP = 16
+QUARTERS = 4
 
 BF16, F32, U16 = mybir.dt.bfloat16, mybir.dt.float32, mybir.dt.uint16
 ADD = mybir.AluOpType.add
@@ -17,50 +19,78 @@ def tile_lookup_res_add_relu_kernel(tc, tab, base, w, b, offs, out):
     vectors = base.shape[1]
     features = w.shape[1]
     blocks, pieces = rows // P, vectors // PIECE
+    units = [(r, c) for r in range(blocks) for c in range(pieces)]
 
     with (
         tc.tile_pool(name="held", bufs=1) as held,
         tc.psum_pool(name="psum", bufs=1) as psum,
     ):
         offsets = held.tile([P, offs.shape[1]], U16, name="offsets")
-        nc.sync.dma_start(offsets[:], offs)
+        windows = {(r, d): held.tile([P, codewords], F32, name=f"window_{r}_{d}")
+                   for r in range(blocks) for d in range(stages)}
+        base_f32 = {(r, c): held.tile([P, PIECE], F32, name=f"base_f32_{r}_{c}") for r, c in units}
+        partial = {(r, c): held.tile([P, PIECE], F32, name=f"partial_{r}_{c}") for r, c in units}
+        w_f32 = held.tile([P, blocks, features], F32, name="w_f32")
+        bias = held.tile([P, 1], F32, name="bias")
+        banks = [psum.tile([P, HALF], F32, name=f"bank_{h}") for h in range(vectors // HALF)]
 
-        windows, sums = {}, {}
-        for r in range(blocks):
-            block = slice(r * P, (r + 1) * P)
-            for d in range(stages):
-                tab_bf = held.tile([P, codewords], BF16, name=f"tab_bf_{r}_{d}")
-                nc.sync.dma_start(tab_bf[:], tab[d, block, :])
-                windows[r, d] = held.tile([P, codewords], F32, name=f"window_{r}_{d}")
-                nc.scalar.copy(windows[r, d][:], tab_bf[:])
-                if d == 0:
-                    base_bf = held.tile([P, vectors], BF16, name=f"base_bf_{r}")
-                    nc.sync.dma_start(base_bf[:], base[block, :])
-                    sums[r, 0] = held.tile([P, vectors], F32, name=f"base_f32_{r}")
-                    nc.scalar.copy(sums[r, 0][:], base_bf[:])
-                sums[r, d + 1] = held.tile([P, vectors], F32, name=f"sum_{r}_{d}")
-            if r == 0:
+        def prepare_base(r, c):
+            base_bf = held.tile([P, PIECE], BF16, name=f"base_bf_{r}_{c}")
+            nc.sync.dma_start(base_bf[:], base[r * P : (r + 1) * P, c * PIECE : (c + 1) * PIECE])
+            nc.scalar.copy(base_f32[r, c][:], base_bf[:])
+
+        def prepare_window(r, d):
+            tab_bf = held.tile([P, codewords], BF16, name=f"tab_bf_{r}_{d}")
+            nc.sync.dma_start(tab_bf[:], tab[d, r * P : (r + 1) * P, :])
+            nc.scalar.copy(windows[r, d][:], tab_bf[:])
+
+        def prepare_first_window():
+            width = codewords // QUARTERS
+            for q in range(QUARTERS):
+                part = slice(q * width, (q + 1) * width)
+                quarter_bf = held.tile([P, width], BF16, name=f"quarter_bf_{q}")
+                nc.sync.dma_start(quarter_bf[:], tab[0, 0:P, part])
+                if q == 0:
+                    nc.scalar.copy(windows[0, 0][:, part], quarter_bf[:])
+                else:
+                    nc.vector.tensor_copy(windows[0, 0][:, part], quarter_bf[:])
+
+        def look_up_and_add(total, r, d, c, addend):
+            first = (d * vectors + c * PIECE) // GROUP
+            picked = windows[r, d][:].indirect(offsets[:, first : first + PIECE // GROUP])
+            nc.vector.tensor_tensor(total[:], picked, addend[:], ADD)
+
+        prepare_base(0, 0)
+        prepare_first_window()
+        nc.sync.dma_start(offsets[:], offs)
+        for c in range(1, pieces):
+            prepare_base(0, c)
+        prepare_window(0, 1)
+        for r in range(1, blocks):
+            prepare_window(r, 0)
+            prepare_base(r, 0)
+            prepare_base(r, 1)
+            prepare_window(r, 1)
+            prepare_base(r, 2)
+            if r == 1:
                 w_bf = held.tile([P, blocks, features], BF16, name="w_bf")
                 nc.sync.dma_start(w_bf[:], w.rearrange("(r p) m -> p r m", p=P))
-                w_f32 = held.tile([P, blocks, features], F32, name="w_f32")
                 nc.scalar.copy(w_f32[:], w_bf[:])
-                bias = held.tile([P, 1], F32, name="bias")
                 nc.sync.dma_start(bias[:], b)
 
-        banks = [psum.tile([P, PIECE], F32, name=f"bank_{c}") for c in range(pieces)]
-        for r in range(blocks):
-            for d in range(stages):
-                for c in range(pieces):
-                    columns = slice(c * PIECE, (c + 1) * PIECE)
-                    first = (d * vectors + c * PIECE) // GROUP
-                    picked = windows[r, d][:].indirect(offsets[:, first : first + PIECE // GROUP])
-                    nc.vector.tensor_tensor(sums[r, d + 1][:, columns], picked, sums[r, d][:, columns], ADD)
-            for c in range(pieces):
-                columns = slice(c * PIECE, (c + 1) * PIECE)
-                nc.tensor.matmul(banks[c][:], w_f32[:, r, :], sums[r, stages][:, columns],
-                                 start=r == 0, stop=r == blocks - 1)
-
         for c in range(pieces):
-            result = held.tile([P, PIECE], F32, name=f"result_{c}")
-            nc.scalar.activation(result[:], banks[c][:], RELU, bias=bias[:])
-            nc.sync.dma_start(out[:, c * PIECE : (c + 1) * PIECE], result[:])
+            look_up_and_add(partial[0, c], 0, 0, c, base_f32[0, c])
+        for u, (r, c) in enumerate(units):
+            if pieces <= u + 1 < len(units):
+                next_r, next_c = units[u + 1]
+                look_up_and_add(partial[next_r, next_c], next_r, 0, next_c, base_f32[next_r, next_c])
+            x = held.tile([P, PIECE], F32, name=f"x_{r}_{c}")
+            look_up_and_add(x, r, 1, c, partial[r, c])
+            for half in range(PIECE // HALF):
+                h = c * (PIECE // HALF) + half
+                nc.tensor.matmul(banks[h][:], w_f32[:, r, :], x[:, half * HALF : (half + 1) * HALF],
+                                 start=r == 0, stop=r == blocks - 1)
+                if r == blocks - 1:
+                    result = held.tile([P, HALF], F32, name=f"result_{h}")
+                    nc.scalar.activation(result[:], banks[h][:], RELU, bias=bias[:])
+                    nc.sync.dma_start(out[:, h * HALF : (h + 1) * HALF], result[:])

@@ -40,9 +40,12 @@ def tile_lookup_res_add_relu_kernel(tc, tab, base, w, b, offs, out):
             nc.scalar.copy(base_f32[r, c][:], base_bf[:])
 
         def prepare_window(r, d):
-            tab_bf = held.tile([P, codewords], BF16, name=f"tab_bf_{r}_{d}")
-            nc.sync.dma_start(tab_bf[:], tab[d, r * P : (r + 1) * P, :])
-            nc.scalar.copy(windows[r, d][:], tab_bf[:])
+            width = codewords // 2
+            for side in range(2):
+                part = slice(side * width, (side + 1) * width)
+                tab_bf = held.tile([P, width], BF16, name=f"tab_bf_{r}_{d}_{side}")
+                nc.sync.dma_start(tab_bf[:], tab[d, r * P : (r + 1) * P, part])
+                nc.scalar.copy(windows[r, d][:, part], tab_bf[:])
 
         def prepare_first_window():
             width = codewords // QUARTERS
@@ -67,30 +70,35 @@ def tile_lookup_res_add_relu_kernel(tc, tab, base, w, b, offs, out):
             prepare_base(0, c)
         prepare_window(0, 1)
         for r in range(1, blocks):
+            early = pieces if r < blocks - 1 else pieces - 1
             prepare_window(r, 0)
-            prepare_base(r, 0)
-            prepare_base(r, 1)
+            for c in range(early):
+                prepare_base(r, c)
             prepare_window(r, 1)
-            prepare_base(r, 2)
+            for c in range(early, pieces):
+                prepare_base(r, c)
             if r == 1:
                 w_bf = held.tile([P, blocks, features], BF16, name="w_bf")
                 nc.sync.dma_start(w_bf[:], w.rearrange("(r p) m -> p r m", p=P))
                 nc.scalar.copy(w_f32[:], w_bf[:])
                 nc.sync.dma_start(bias[:], b)
 
-        for c in range(pieces):
-            look_up_and_add(partial[0, c], 0, 0, c, base_f32[0, c])
-        for u, (r, c) in enumerate(units):
-            if pieces <= u + 1 < len(units):
-                next_r, next_c = units[u + 1]
-                look_up_and_add(partial[next_r, next_c], next_r, 0, next_c, base_f32[next_r, next_c])
-            x = held.tile([P, PIECE], F32, name=f"x_{r}_{c}")
-            look_up_and_add(x, r, 1, c, partial[r, c])
-            for half in range(PIECE // HALF):
-                h = c * (PIECE // HALF) + half
-                nc.tensor.matmul(banks[h][:], w_f32[:, r, :], x[:, half * HALF : (half + 1) * HALF],
-                                 start=r == 0, stop=r == blocks - 1)
-                if r == blocks - 1:
-                    result = held.tile([P, HALF], F32, name=f"result_{h}")
-                    nc.scalar.activation(result[:], banks[h][:], RELU, bias=bias[:])
-                    nc.sync.dma_start(out[:, h * HALF : (h + 1) * HALF], result[:])
+        def run_pieces(r, chosen):
+            for c in chosen:
+                look_up_and_add(partial[r, c], r, 0, c, base_f32[r, c])
+            for c in chosen:
+                x = held.tile([P, PIECE], F32, name=f"x_{r}_{c}")
+                look_up_and_add(x, r, 1, c, partial[r, c])
+                for half in range(PIECE // HALF):
+                    h = c * (PIECE // HALF) + half
+                    nc.tensor.matmul(banks[h][:], w_f32[:, r, :], x[:, half * HALF : (half + 1) * HALF],
+                                     start=r == 0, stop=r == blocks - 1)
+                    if r == blocks - 1:
+                        result = held.tile([P, HALF], F32, name=f"result_{h}")
+                        nc.scalar.activation(result[:], banks[h][:], RELU, bias=bias[:])
+                        nc.sync.dma_start(out[:, h * HALF : (h + 1) * HALF], result[:])
+
+        for r in range(blocks - 1):
+            run_pieces(r, range(pieces))
+        run_pieces(blocks - 1, range(pieces - 1))
+        run_pieces(blocks - 1, range(pieces - 1, pieces))

import concourse.mybir as mybir

P = 128
PIECE = 512
HALF = 256
GROUP = 16
QUARTERS = 4

BF16, F32, U16 = mybir.dt.bfloat16, mybir.dt.float32, mybir.dt.uint16
ADD = mybir.AluOpType.add
RELU = mybir.ActivationFunctionType.Relu

FLOPS = 2 * 512 * 128 * 1536


def tile_lookup_res_add_relu_kernel(tc, tab, base, w, b, offs, out):
    nc = tc.nc
    stages, rows, codewords = tab.shape
    vectors = base.shape[1]
    features = w.shape[1]
    blocks, pieces = rows // P, vectors // PIECE
    units = [(r, c) for r in range(blocks) for c in range(pieces)]

    with (
        tc.tile_pool(name="held", bufs=1) as held,
        tc.psum_pool(name="psum", bufs=1) as psum,
    ):
        offsets = held.tile([P, offs.shape[1]], U16, name="offsets")
        windows = {(r, d): held.tile([P, codewords], F32, name=f"window_{r}_{d}")
                   for r in range(blocks) for d in range(stages)}
        base_f32 = {(r, c): held.tile([P, PIECE], F32, name=f"base_f32_{r}_{c}") for r, c in units}
        partial = {(r, c): held.tile([P, PIECE], F32, name=f"partial_{r}_{c}") for r, c in units}
        w_f32 = held.tile([P, blocks, features], F32, name="w_f32")
        bias = held.tile([P, 1], F32, name="bias")
        banks = [psum.tile([P, HALF], F32, name=f"bank_{h}") for h in range(vectors // HALF)]

        def prepare_base(r, c):
            base_bf = held.tile([P, PIECE], BF16, name=f"base_bf_{r}_{c}")
            nc.sync.dma_start(base_bf[:], base[r * P : (r + 1) * P, c * PIECE : (c + 1) * PIECE])
            nc.scalar.copy(base_f32[r, c][:], base_bf[:])

        def prepare_window(r, d):
            width = codewords // 2
            for side in range(2):
                part = slice(side * width, (side + 1) * width)
                tab_bf = held.tile([P, width], BF16, name=f"tab_bf_{r}_{d}_{side}")
                nc.sync.dma_start(tab_bf[:], tab[d, r * P : (r + 1) * P, part])
                nc.scalar.copy(windows[r, d][:, part], tab_bf[:])

        def prepare_first_window():
            width = codewords // QUARTERS
            for q in range(QUARTERS):
                part = slice(q * width, (q + 1) * width)
                quarter_bf = held.tile([P, width], BF16, name=f"quarter_bf_{q}")
                nc.sync.dma_start(quarter_bf[:], tab[0, 0:P, part])
                if q == 0:
                    nc.scalar.copy(windows[0, 0][:, part], quarter_bf[:])
                else:
                    nc.vector.tensor_copy(windows[0, 0][:, part], quarter_bf[:])

        def look_up_and_add(total, r, d, c, addend):
            first = (d * vectors + c * PIECE) // GROUP
            picked = windows[r, d][:].indirect(offsets[:, first : first + PIECE // GROUP])
            nc.vector.tensor_tensor(total[:], picked, addend[:], ADD)

        prepare_base(0, 0)
        prepare_first_window()
        nc.sync.dma_start(offsets[:], offs)
        for c in range(1, pieces):
            prepare_base(0, c)
        prepare_window(0, 1)
        for r in range(1, blocks):
            early = pieces if r < blocks - 1 else pieces - 1
            prepare_window(r, 0)
            for c in range(early):
                prepare_base(r, c)
            prepare_window(r, 1)
            for c in range(early, pieces):
                prepare_base(r, c)
            if r == 1:
                w_bf = held.tile([P, blocks, features], BF16, name="w_bf")
                nc.sync.dma_start(w_bf[:], w.rearrange("(r p) m -> p r m", p=P))
                nc.scalar.copy(w_f32[:], w_bf[:])
                nc.sync.dma_start(bias[:], b)

        def run_pieces(r, chosen):
            for c in chosen:
                look_up_and_add(partial[r, c], r, 0, c, base_f32[r, c])
            for c in chosen:
                x = held.tile([P, PIECE], F32, name=f"x_{r}_{c}")
                look_up_and_add(x, r, 1, c, partial[r, c])
                for half in range(PIECE // HALF):
                    h = c * (PIECE // HALF) + half
                    nc.tensor.matmul(banks[h][:], w_f32[:, r, :], x[:, half * HALF : (half + 1) * HALF],
                                     start=r == 0, stop=r == blocks - 1)
                    if r == blocks - 1:
                        result = held.tile([P, HALF], F32, name=f"result_{h}")
                        nc.scalar.activation(result[:], banks[h][:], RELU, bias=bias[:])
                        nc.sync.dma_start(out[:, h * HALF : (h + 1) * HALF], result[:])

        for r in range(blocks - 1):
            run_pieces(r, range(pieces))
        run_pieces(blocks - 1, range(pieces - 1))
        run_pieces(blocks - 1, range(pieces - 1, pieces))
